import numpy as np
import ml_dtypes


def mxq(x, axis, fmt="e4m3"):
    dtype, down = {"e4m3": (ml_dtypes.float8_e4m3fn, 7), "e5m2": (ml_dtypes.float8_e5m2, 14)}[fmt]
    v = np.moveaxis(np.asarray(x, np.float32).astype(ml_dtypes.bfloat16).astype(np.float64), axis, -1)
    blocks = v.reshape(v.shape[:-1] + (-1, 32))
    amax = np.abs(blocks).max(-1, keepdims=True)
    byte = np.maximum(np.where(amax > 0, np.frexp(amax)[1] - 1 + 127, 0) - down, 1)
    scale = np.exp2(byte - 127.0)
    codes = (blocks / scale).astype(np.float32).astype(dtype).astype(np.float64)
    return np.moveaxis((codes * scale).reshape(v.shape), -1, axis)


WIDE = False


def mx_kscale(k):
    if not WIDE:
        return np.ones(k)
    levels = np.array([10, -10, 5, -5, 0])
    if k % 512:
        return np.exp2(np.random.permutation(np.resize(levels, k // 32))).repeat(32)
    a = np.empty((k // 512, 16))
    for p in range(k // 512):
        a[p, :8] = np.random.permutation(np.resize(levels, 8))
        for g in range(8):
            far = levels[np.abs(levels - a[p, g]) >= 10]
            a[p, g + 8] = far[np.random.randint(len(far))]
    return np.exp2(a.ravel()).repeat(32)


def f64(x):
    return np.asarray(x).astype(np.float64)


def striped(idx):
    return np.tile(np.asarray(idx).reshape(-1, 16).T, (8, 1)).astype(np.uint16)


def unstriped(offs):
    return offs[:16].T.reshape(-1).astype(np.int64)


E2M1 = np.array([0.0, 0.5, 1.0, 1.5, 2.0, 3.0, 4.0, 6.0, -0.0, -0.5, -1.0, -1.5, -2.0, -3.0, -4.0, -6.0])


def pack_weight(w, fmt):
    k, n = w.shape
    w = f64(np.asarray(w, np.float32).astype(ml_dtypes.bfloat16)).reshape(k // 32, 32, n)
    amax = np.abs(w).max(1)
    if fmt == "e4m3":
        byte = np.frexp(amax)[1] - 1 + 127 - 7
    else:
        mant, ex = np.frexp(amax / 6.0)
        byte = np.where(mant > 0.5, ex, ex - 1) + 127
    byte = np.clip(np.where(amax > 0, byte, 1), 1, 254)
    scaled = (w * np.exp2(127.0 - byte)[:, None, :]).reshape(k, n).astype(np.float32)
    by_word = np.ascontiguousarray(scaled.reshape(k // 512, 128, 4, n).transpose(0, 1, 3, 2))
    if fmt == "e4m3":
        words = by_word.astype(ml_dtypes.float8_e4m3fn).view(np.uint8)
    else:
        c = by_word.astype(ml_dtypes.float4_e2m1fn).view(np.uint8) & 0xF
        words = (c[..., 0::2] | (c[..., 1::2] << 4)).reshape(k // 512, 128, 2 * n)
    return np.ascontiguousarray(words), np.ascontiguousarray(byte.astype(np.uint8).reshape(k // 512, 16, n))


def unpack_weight(words, scales, fmt):
    g, _, n = scales.shape
    words = np.ascontiguousarray(words).reshape(g, 128, n, -1)
    if fmt == "e4m3":
        vals = words.view(ml_dtypes.float8_e4m3fn).astype(np.float64)
    else:
        nib = np.empty((g, 128, n, 4), np.uint8)
        nib[..., 0::2] = words & 0xF
        nib[..., 1::2] = words >> 4
        vals = E2M1[nib]
    vals = vals * np.repeat(np.exp2(scales.astype(np.float64) - 127.0), 8, axis=1)[..., None]
    return vals.transpose(0, 1, 3, 2).reshape(g * 512, n)


K, T, V, J, N, E = 512, 1024, 512, 256, 256, 512


def setup_inputs():
    n = np.random.standard_normal
    idx = np.random.permutation(T)[:J]
    idx2 = np.random.permutation(V)[:J]
    idx3 = np.random.permutation(E)[:J]
    fk = mx_kscale(K)
    wp = pack_weight(n((K, N)) * 1 / np.sqrt(K) / fk[:, None], "e4m3")
    return {
        "ca": (np.random.randint(-7, 8, (K, T)).astype(np.float64)).astype(np.float32),
        "cb": (np.random.randint(-7, 8, (K, V)).astype(np.float64)).astype(np.float32),
        "sa": (np.random.uniform(0.1, 0.4, (K, 1)) * fk[:, None]).astype(np.float32),
        "sb": (np.random.uniform(0.1, 0.4, (K, 1)) * fk[:, None]).astype(np.float32),
        "w_words": wp[0],
        "w_scales": wp[1],
        "so": (np.random.uniform(0.5, 1.6, (N, 1))).astype(np.float32),
        "offs": striped(idx),
        "offs2": striped(idx2),
        "offs3": striped(idx3),
    }


def reference(ca, cb, sa, sb, w_words, w_scales, so, offs, offs2, offs3):
    idx = unstriped(offs)
    idx2 = unstriped(offs2)
    idx3 = unstriped(offs3)
    wu = unpack_weight(w_words, w_scales, "e4m3")
    x1 = f64(ca)[:, idx] * f64(sa)
    x2 = f64(cb)[:, idx2] * f64(sb)
    x1q = mxq(x1, 0, "e4m3")
    x2q = mxq(x2, 0, "e4m3")
    p = wu.T @ x1q + wu.T @ x2q
    y = np.zeros((N, E))
    y[:, idx3] = p * f64(so)
    return y

@@ -1,0 +1,129 @@
+from contextlib import ExitStack
+
+import concourse.mybir as mybir
+
+K, T, V, J, N, E = 512, 1024, 512, 256, 256, 512
+FLOPS = 2 * 2 * K * N * J
+
+F32 = mybir.dt.float32
+BF16 = mybir.dt.bfloat16
+I32 = mybir.dt.int32
+U32 = mybir.dt.uint32
+U16 = mybir.dt.uint16
+U8 = mybir.dt.uint8
+FP8X4 = mybir.dt.float8_e4m3fn_x4
+COPY = mybir.ActivationFunctionType.Copy
+
+P = 128
+PACK = 4
+STRIPE = 16
+HALF = J // 2
+
+
+def tile_list_twocodebooks_kernel(tc, ca, cb, sa, sb, w_words, w_scales, so, offs, offs2, offs3, out):
+    nc = tc.nc
+    with ExitStack() as ctx:
+        keep = ctx.enter_context(tc.tile_pool(name="keep", bufs=1))
+        psum = ctx.enter_context(tc.psum_pool(name="psum", bufs=1))
+
+        idx_a = keep.tile([P, J // STRIPE], U16, name="idx_a")
+        idx_b = keep.tile([P, J // STRIPE], U16, name="idx_b")
+        idx_out = keep.tile([P, J // STRIPE], U16, name="idx_out")
+        step_a = keep.tile([P, PACK], F32, name="step_a")
+        step_b = keep.tile([P, PACK], F32, name="step_b")
+        gain = keep.tile([P, N // P], F32, name="gain")
+        rows_a = [keep.tile([P, T], F32, name="rows_a%d" % r) for r in range(PACK)]
+        rows_b = [keep.tile([P, V], F32, name="rows_b%d" % r) for r in range(PACK)]
+        w_codes = keep.tile([P, N], U32, name="w_codes", align_bytes=64)
+        w_plane = keep.tile([P, N], U8, name="w_plane", align_bytes=64)
+        w_stage = keep.tile([PACK, PACK, N // 4], I32, name="w_stage")
+        pages = [keep.tile([P, E], F32, name="page%d" % h) for h in range(N // P)]
+
+        ca_rows = ca.rearrange("(p r) t -> p r t", r=PACK)
+        cb_rows = cb.rearrange("(p r) v -> p r v", r=PACK)
+
+        nc.scalar.dma_start(step_b[:], sb.rearrange("(p r) o -> p (r o)", r=PACK))
+        nc.scalar.dma_start(step_a[:], sa.rearrange("(p r) o -> p (r o)", r=PACK))
+        nc.sync.dma_start(idx_b[:], offs2)
+        for r in range(PACK):
+            nc.sync.dma_start(rows_b[r][:], cb_rows[:, r, :])
+        nc.sync.dma_start(rows_a[0][:], ca_rows[:, 0, :])
+        nc.sync.dma_start(idx_a[:], offs)
+        for r in range(1, PACK):
+            nc.sync.dma_start(rows_a[r][:], ca_rows[:, r, :])
+        nc.sync.dma_start(w_codes[:].bitcast(I32), w_words[0].rearrange("p n t -> p (n t)").bitcast(I32))
+        nc.sync.dma_start(idx_out[:], offs3)
+        nc.gpsimd.dma_start(w_stage[:], w_scales[0].bitcast(I32).rearrange("(q r) n -> r q n", r=PACK))
+        with nc.allow_non_contiguous_dma(reason="one float a partition"):
+            nc.sync.dma_start(gain[:], so.rearrange("(h p) o -> p (h o)", p=P))
+
+        nc.vector.memset(w_plane[:].bitcast(I32), 0)
+        for page in pages:
+            nc.vector.memset(page[:], 0.0)
+        for q in range(PACK):
+            nc.vector.tensor_copy(w_plane[:].bitcast(I32)[32 * q : 32 * q + PACK, :], w_stage[:, q, :])
+
+        def operand(name):
+            x = keep.tile([P, PACK * J], BF16, name="x_" + name, align_bytes=64)
+            codes = keep.tile([P, J], U32, name="codes_" + name, align_bytes=64)
+            plane = keep.tile([P, J], U8, name="plane_" + name, align_bytes=64)
+            return x, codes, plane
+
+        x_a, codes_a, plane_a = operand("a")
+        x_b, codes_b, plane_b = operand("b")
+
+        def fetch(x, rows, step, idx, r, j0, j1):
+            nc.scalar.activation(
+                out=x[:, PACK * j0 + r : PACK * j1 : PACK],
+                in_=rows[r][:].indirect(idx[:, j0 // STRIPE : j1 // STRIPE]),
+                func=COPY,
+                scale=step[:, r : r + 1],
+            )
+
+        def quantize(x, codes, plane, j0, j1):
+            nc.vector.quantize_mx(
+                out=codes[:, j0:j1].bitcast(FP8X4), scales=plane[:, j0:j1], in_=x[:, PACK * j0 : PACK * j1]
+            )
+
+        halves = [(0, HALF), (HALF, J)]
+        banks = [[psum.tile([P, 512], F32, name="acc%d_%d" % (h, u)) for u in range(2)] for h in range(N // P)]
+        sums = [keep.tile([P, J], F32, name="sums%d" % h) for h in range(N // P)]
+
+        def multiply(codes, plane, h, u, first):
+            j0, j1 = halves[u]
+            nc.tensor.matmul_mx(
+                out=banks[h][u][:, 0:HALF],
+                lhsT=w_codes[:, h * P : (h + 1) * P].bitcast(FP8X4),
+                lhsT_scale=w_plane[:, h * P : (h + 1) * P],
+                rhs=codes[:, j0:j1].bitcast(FP8X4),
+                rhs_scale=plane[:, j0:j1],
+                start=first,
+                stop=not first,
+            )
+
+        for r in range(PACK):
+            fetch(x_b, rows_b, step_b, idx_b, r, 0, J)
+        quantize(x_b, codes_b, plane_b, 0, J)
+        for r in range(PACK - 1):
+            fetch(x_a, rows_a, step_a, idx_a, r, 0, J)
+        for u in range(2):
+            for h in range(N // P):
+                multiply(codes_b, plane_b, h, u, True)
+        for u, (j0, j1) in enumerate(halves):
+            fetch(x_a, rows_a, step_a, idx_a, PACK - 1, j0, j1)
+            quantize(x_a, codes_a, plane_a, j0, j1)
+            for h in range(N // P):
+                multiply(codes_a, plane_a, h, u, False)
+        for u, (j0, j1) in enumerate(halves):
+            for h in range(N // P):
+                nc.vector.tensor_copy(sums[h][:, j0:j1], banks[h][u][:, 0:HALF])
+        for j0, j1 in halves:
+            nc.scalar.activation(
+                out=pages[0][:].indirect(idx_out[:, j0 // STRIPE : j1 // STRIPE]),
+                in_=sums[0][:, j0:j1],
+                func=COPY,
+                scale=gain[:, 0:1],
+            )
+        nc.sync.dma_start(out[0:P, :], pages[0][:])
+        nc.scalar.activation(out=pages[1][:].indirect(idx_out[:]), in_=sums[1][:], func=COPY, scale=gain[:, 1:2])
+        nc.sync.dma_start(out[P:N, :], pages[1][:])

@@ -57,6 +57,10 @@ def tile_list_twocodebooks_kernel(tc, ca, cb, sa, sb, w_words, w_scales, so, off
         with nc.allow_non_contiguous_dma(reason="one float a partition"):
             nc.sync.dma_start(gain[:], so.rearrange("(h p) o -> p (h o)", p=P))
 
+        warm_in = keep.tile([P, 1], F32, name="warm_in")
+        warm_out = keep.tile([P, 1], F32, name="warm_out")
+        nc.vector.memset(warm_in[:], 0.0)
+        nc.scalar.activation(out=warm_out[:], in_=warm_in[:], func=COPY)
         nc.vector.memset(w_plane[:].bitcast(I32), 0)
         for page in pages:
             nc.vector.memset(page[:], 0.0)

@@ -29,43 +29,58 @@ def tile_list_twocodebooks_kernel(tc, ca, cb, sa, sb, w_words, w_scales, so, off
         idx_a = keep.tile([P, J // STRIPE], U16, name="idx_a")
         idx_b = keep.tile([P, J // STRIPE], U16, name="idx_b")
         idx_out = keep.tile([P, J // STRIPE], U16, name="idx_out")
-        step_a = keep.tile([P, PACK], F32, name="step_a")
+        sa_rows = keep.tile([P, P], F32, name="sa_rows")
+        sa_dealt = keep.tile([P, P], F32, name="sa_dealt", align_bytes=64)
+        step_a = keep.tile([P, P], F32, name="step_a", align_bytes=64)
         step_b = keep.tile([P, PACK], F32, name="step_b")
-        gain = keep.tile([P, N // P], F32, name="gain")
+        gain_rows = keep.tile([P, P], F32, name="gain_rows", align_bytes=64)
+        gain = keep.tile([P, P], F32, name="gain", align_bytes=64)
         rows_a = [keep.tile([P, T], F32, name="rows_a%d" % r) for r in range(PACK)]
-        rows_b = [keep.tile([P, V], F32, name="rows_b%d" % r) for r in range(PACK)]
+        rows_b = [keep.tile([P, 2 * V if r == 2 else V], F32, name="rows_b%d" % r) for r in range(PACK)]
         w_codes = keep.tile([P, N], U32, name="w_codes", align_bytes=64)
         w_plane = keep.tile([P, N], U8, name="w_plane", align_bytes=64)
-        w_stage = keep.tile([PACK, PACK, N // 4], I32, name="w_stage")
         pages = [keep.tile([P, E], F32, name="page%d" % h) for h in range(N // P)]
 
         ca_rows = ca.rearrange("(p r) t -> p r t", r=PACK)
         cb_rows = cb.rearrange("(p r) v -> p r v", r=PACK)
 
-        nc.scalar.dma_start(step_b[:], sb.rearrange("(p r) o -> p (r o)", r=PACK))
-        nc.scalar.dma_start(step_a[:], sa.rearrange("(p r) o -> p (r o)", r=PACK))
-        nc.sync.dma_start(idx_b[:], offs2)
-        for r in range(PACK):
-            nc.sync.dma_start(rows_b[r][:], cb_rows[:, r, :])
-        nc.sync.dma_start(rows_a[0][:], ca_rows[:, 0, :])
-        nc.sync.dma_start(idx_a[:], offs)
-        for r in range(1, PACK):
-            nc.sync.dma_start(rows_a[r][:], ca_rows[:, r, :])
-        nc.sync.dma_start(w_codes[:].bitcast(I32), w_words[0].rearrange("p n t -> p (n t)").bitcast(I32))
-        nc.sync.dma_start(idx_out[:], offs3)
-        nc.gpsimd.dma_start(w_stage[:], w_scales[0].bitcast(I32).rearrange("(q r) n -> r q n", r=PACK))
-        with nc.allow_non_contiguous_dma(reason="one float a partition"):
-            nc.sync.dma_start(gain[:], so.rearrange("(h p) o -> p (h o)", p=P))
-
         warm_in = keep.tile([P, 1], F32, name="warm_in")
         warm_out = keep.tile([P, 1], F32, name="warm_out")
         nc.vector.memset(warm_in[:], 0.0)
         nc.scalar.activation(out=warm_out[:], in_=warm_in[:], func=COPY)
+        nc.sync.dma_start(rows_b[0][:], cb_rows[:, 0, :])
+        nc.sync.dma_start(idx_b[:], offs2)
+        nc.sync.dma_start(step_b[:], sb.rearrange("(p r) o -> p (r o)", r=PACK))
+        nc.sync.dma_start(rows_b[1][:], cb_rows[:, 1, :])
+        nc.sync.dma_start(sa_rows[0:P:32, :], sa.rearrange("(q k) o -> q (k o)", q=4))
+        nc.sync.dma_start(rows_b[2][:], cb_rows[:, 2:4, :].rearrange("p r v -> p (r v)"))
+        nc.sync.dma_start(rows_a[0][:], ca_rows[:, 0, :])
+        nc.sync.dma_start(idx_a[:], offs)
+        nc.vector.memset(gain_rows[:], 0.0)
+        nc.sync.dma_start(
+            gain_rows[0:P:32, 0:64].rearrange("q (h i) -> q h i", i=32),
+            so.rearrange("(h q i) o -> q h (i o)", q=4, i=32),
+        )
+        for r in range(1, PACK):
+            nc.sync.dma_start(rows_a[r][:], ca_rows[:, r, :])
         nc.vector.memset(w_plane[:].bitcast(I32), 0)
+        for q in range(4):
+            nc.sync.dma_start(
+                w_plane[:].bitcast(I32)[32 * q : 32 * q + 4, :], w_scales[0].bitcast(I32)[4 * q : 4 * q + 4, :]
+            )
+        nc.sync.dma_start(w_codes[:].bitcast(I32), w_words[0].rearrange("p n t -> p (n t)").bitcast(I32))
+        nc.sync.dma_start(idx_out[:], offs3)
+
+        nc.vector.memset(sa_dealt[:], 0.0)
         for page in pages:
             nc.vector.memset(page[:], 0.0)
-        for q in range(PACK):
-            nc.vector.tensor_copy(w_plane[:].bitcast(I32)[32 * q : 32 * q + PACK, :], w_stage[:, q, :])
+        for q in range(0, P, 32):
+            nc.vector.tensor_copy(
+                sa_dealt[q : q + 1, :].rearrange("p (r i) -> p r i", r=PACK),
+                sa_rows[q : q + 1, :].rearrange("p (i r) -> p r i", r=PACK),
+            )
+        nc.vector.transpose(step_a[:], sa_dealt[:])
+        nc.vector.tensor_copy(rows_b[3][:], rows_b[2][:, V : 2 * V])
 
         def operand(name):
             x = keep.tile([P, PACK * J], BF16, name="x_" + name, align_bytes=64)
@@ -76,12 +91,12 @@ def tile_list_twocodebooks_kernel(tc, ca, cb, sa, sb, w_words, w_scales, so, off
         x_a, codes_a, plane_a = operand("a")
         x_b, codes_b, plane_b = operand("b")
 
-        def fetch(x, rows, step, idx, r, j0, j1):
+        def fetch(x, rows, step, pitch, idx, r, j0, j1):
             nc.scalar.activation(
                 out=x[:, PACK * j0 + r : PACK * j1 : PACK],
                 in_=rows[r][:].indirect(idx[:, j0 // STRIPE : j1 // STRIPE]),
                 func=COPY,
-                scale=step[:, r : r + 1],
+                scale=step[:, pitch * r : pitch * r + 1],
             )
 
         def quantize(x, codes, plane, j0, j1):
@@ -90,13 +105,12 @@ def tile_list_twocodebooks_kernel(tc, ca, cb, sa, sb, w_words, w_scales, so, off
             )
 
         halves = [(0, HALF), (HALF, J)]
-        banks = [[psum.tile([P, 512], F32, name="acc%d_%d" % (h, u)) for u in range(2)] for h in range(N // P)]
+        banks = [psum.tile([P, J], F32, name="acc%d" % h) for h in range(N // P)]
         sums = [keep.tile([P, J], F32, name="sums%d" % h) for h in range(N // P)]
 
-        def multiply(codes, plane, h, u, first):
-            j0, j1 = halves[u]
+        def multiply(codes, plane, h, j0, j1, first):
             nc.tensor.matmul_mx(
-                out=banks[h][u][:, 0:HALF],
+                out=banks[h][:, j0:j1],
                 lhsT=w_codes[:, h * P : (h + 1) * P].bitcast(FP8X4),
                 lhsT_scale=w_plane[:, h * P : (h + 1) * P],
                 rhs=codes[:, j0:j1].bitcast(FP8X4),
@@ -106,28 +120,25 @@ def tile_list_twocodebooks_kernel(tc, ca, cb, sa, sb, w_words, w_scales, so, off
             )
 
         for r in range(PACK):
-            fetch(x_b, rows_b, step_b, idx_b, r, 0, J)
+            fetch(x_b, rows_b, step_b, 1, idx_b, r, 0, J)
         quantize(x_b, codes_b, plane_b, 0, J)
+        nc.vector.transpose(gain[:], gain_rows[:])
         for r in range(PACK - 1):
-            fetch(x_a, rows_a, step_a, idx_a, r, 0, J)
-        for u in range(2):
-            for h in range(N // P):
-                multiply(codes_b, plane_b, h, u, True)
+            fetch(x_a, rows_a, step_a, 32, idx_a, r, 0, J)
         for u, (j0, j1) in enumerate(halves):
-            fetch(x_a, rows_a, step_a, idx_a, PACK - 1, j0, j1)
+            fetch(x_a, rows_a, step_a, 32, idx_a, PACK - 1, j0, j1)
             quantize(x_a, codes_a, plane_a, j0, j1)
-            for h in range(N // P):
-                multiply(codes_a, plane_a, h, u, False)
-        for u, (j0, j1) in enumerate(halves):
-            for h in range(N // P):
-                nc.vector.tensor_copy(sums[h][:, j0:j1], banks[h][u][:, 0:HALF])
-        for j0, j1 in halves:
+        pieces = [(0, 0, HALF), (1, 0, J), (0, HALF, J)]
+        for h, j0, j1 in pieces:
+            multiply(codes_b, plane_b, h, j0, j1, True)
+            multiply(codes_a, plane_a, h, j0, j1, False)
+            nc.vector.tensor_copy(sums[h][:, j0:j1], banks[h][:, j0:j1])
+        for h, j0, j1 in pieces:
             nc.scalar.activation(
-                out=pages[0][:].indirect(idx_out[:, j0 // STRIPE : j1 // STRIPE]),
-                in_=sums[0][:, j0:j1],
+                out=pages[h][:].indirect(idx_out[:, j0 // STRIPE : j1 // STRIPE]),
+                in_=sums[h][:, j0:j1],
                 func=COPY,
-                scale=gain[:, 0:1],
+                scale=gain[:, 32 * h : 32 * h + 1],
             )
-        nc.sync.dma_start(out[0:P, :], pages[0][:])
-        nc.scalar.activation(out=pages[1][:].indirect(idx_out[:]), in_=sums[1][:], func=COPY, scale=gain[:, 1:2])
-        nc.sync.dma_start(out[P:N, :], pages[1][:])
+            if j1 == J:
+                nc.sync.dma_start(out[h * P : (h + 1) * P, :], pages[h][:])

from contextlib import ExitStack

import concourse.mybir as mybir

K, T, V, J, N, E = 512, 1024, 512, 256, 256, 512
FLOPS = 2 * 2 * K * N * J

F32 = mybir.dt.float32
BF16 = mybir.dt.bfloat16
I32 = mybir.dt.int32
U32 = mybir.dt.uint32
U16 = mybir.dt.uint16
U8 = mybir.dt.uint8
FP8X4 = mybir.dt.float8_e4m3fn_x4
COPY = mybir.ActivationFunctionType.Copy

P = 128
PACK = 4
STRIPE = 16
HALF = J // 2


def tile_list_twocodebooks_kernel(tc, ca, cb, sa, sb, w_words, w_scales, so, offs, offs2, offs3, out):
    nc = tc.nc
    with ExitStack() as ctx:
        keep = ctx.enter_context(tc.tile_pool(name="keep", bufs=1))
        psum = ctx.enter_context(tc.psum_pool(name="psum", bufs=1))

        idx_a = keep.tile([P, J // STRIPE], U16, name="idx_a")
        idx_b = keep.tile([P, J // STRIPE], U16, name="idx_b")
        idx_out = keep.tile([P, J // STRIPE], U16, name="idx_out")
        sa_rows = keep.tile([P, P], F32, name="sa_rows")
        sa_dealt = keep.tile([P, P], F32, name="sa_dealt", align_bytes=64)
        step_a = keep.tile([P, P], F32, name="step_a", align_bytes=64)
        step_b = keep.tile([P, PACK], F32, name="step_b")
        gain_rows = keep.tile([P, P], F32, name="gain_rows", align_bytes=64)
        gain = keep.tile([P, P], F32, name="gain", align_bytes=64)
        rows_a = [keep.tile([P, T], F32, name="rows_a%d" % r) for r in range(PACK)]
        rows_b = [keep.tile([P, 2 * V if r == 2 else V], F32, name="rows_b%d" % r) for r in range(PACK)]
        w_codes = keep.tile([P, N], U32, name="w_codes", align_bytes=64)
        w_plane = keep.tile([P, N], U8, name="w_plane", align_bytes=64)
        pages = [keep.tile([P, E], F32, name="page%d" % h) for h in range(N // P)]

        ca_rows = ca.rearrange("(p r) t -> p r t", r=PACK)
        cb_rows = cb.rearrange("(p r) v -> p r v", r=PACK)

        warm_in = keep.tile([P, 1], F32, name="warm_in")
        warm_out = keep.tile([P, 1], F32, name="warm_out")
        nc.vector.memset(warm_in[:], 0.0)
        nc.scalar.activation(out=warm_out[:], in_=warm_in[:], func=COPY)
        nc.sync.dma_start(rows_b[0][:], cb_rows[:, 0, :])
        nc.sync.dma_start(idx_b[:], offs2)
        nc.sync.dma_start(step_b[:], sb.rearrange("(p r) o -> p (r o)", r=PACK))
        nc.sync.dma_start(rows_b[1][:], cb_rows[:, 1, :])
        nc.sync.dma_start(sa_rows[0:P:32, :], sa.rearrange("(q k) o -> q (k o)", q=4))
        nc.sync.dma_start(rows_b[2][:], cb_rows[:, 2:4, :].rearrange("p r v -> p (r v)"))
        nc.sync.dma_start(rows_a[0][:], ca_rows[:, 0, :])
        nc.sync.dma_start(idx_a[:], offs)
        nc.vector.memset(gain_rows[:], 0.0)
        nc.sync.dma_start(
            gain_rows[0:P:32, 0:64].rearrange("q (h i) -> q h i", i=32),
            so.rearrange("(h q i) o -> q h (i o)", q=4, i=32),
        )
        for r in range(1, PACK):
            nc.sync.dma_start(rows_a[r][:], ca_rows[:, r, :])
        nc.vector.memset(w_plane[:].bitcast(I32), 0)
        for q in range(4):
            nc.sync.dma_start(
                w_plane[:].bitcast(I32)[32 * q : 32 * q + 4, :], w_scales[0].bitcast(I32)[4 * q : 4 * q + 4, :]
            )
        nc.sync.dma_start(w_codes[:].bitcast(I32), w_words[0].rearrange("p n t -> p (n t)").bitcast(I32))
        nc.sync.dma_start(idx_out[:], offs3)

        nc.vector.memset(sa_dealt[:], 0.0)
        for page in pages:
            nc.vector.memset(page[:], 0.0)
        for q in range(0, P, 32):
            nc.vector.tensor_copy(
                sa_dealt[q : q + 1, :].rearrange("p (r i) -> p r i", r=PACK),
                sa_rows[q : q + 1, :].rearrange("p (i r) -> p r i", r=PACK),
            )
        nc.vector.transpose(step_a[:], sa_dealt[:])
        nc.vector.tensor_copy(rows_b[3][:], rows_b[2][:, V : 2 * V])

        def operand(name):
            x = keep.tile([P, PACK * J], BF16, name="x_" + name, align_bytes=64)
            codes = keep.tile([P, J], U32, name="codes_" + name, align_bytes=64)
            plane = keep.tile([P, J], U8, name="plane_" + name, align_bytes=64)
            return x, codes, plane

        x_a, codes_a, plane_a = operand("a")
        x_b, codes_b, plane_b = operand("b")

        def fetch(x, rows, step, pitch, idx, r, j0, j1):
            nc.scalar.activation(
                out=x[:, PACK * j0 + r : PACK * j1 : PACK],
                in_=rows[r][:].indirect(idx[:, j0 // STRIPE : j1 // STRIPE]),
                func=COPY,
                scale=step[:, pitch * r : pitch * r + 1],
            )

        def quantize(x, codes, plane, j0, j1):
            nc.vector.quantize_mx(
                out=codes[:, j0:j1].bitcast(FP8X4), scales=plane[:, j0:j1], in_=x[:, PACK * j0 : PACK * j1]
            )

        halves = [(0, HALF), (HALF, J)]
        banks = [psum.tile([P, J], F32, name="acc%d" % h) for h in range(N // P)]
        sums = [keep.tile([P, J], F32, name="sums%d" % h) for h in range(N // P)]

        def multiply(codes, plane, h, j0, j1, first):
            nc.tensor.matmul_mx(
                out=banks[h][:, j0:j1],
                lhsT=w_codes[:, h * P : (h + 1) * P].bitcast(FP8X4),
                lhsT_scale=w_plane[:, h * P : (h + 1) * P],
                rhs=codes[:, j0:j1].bitcast(FP8X4),
                rhs_scale=plane[:, j0:j1],
                start=first,
                stop=not first,
            )

        for r in range(PACK):
            fetch(x_b, rows_b, step_b, 1, idx_b, r, 0, J)
        quantize(x_b, codes_b, plane_b, 0, J)
        nc.vector.transpose(gain[:], gain_rows[:])
        for r in range(PACK - 1):
            fetch(x_a, rows_a, step_a, 32, idx_a, r, 0, J)
        for u, (j0, j1) in enumerate(halves):
            fetch(x_a, rows_a, step_a, 32, idx_a, PACK - 1, j0, j1)
            quantize(x_a, codes_a, plane_a, j0, j1)
        pieces = [(0, 0, HALF), (1, 0, J), (0, HALF, J)]
        for h, j0, j1 in pieces:
            multiply(codes_b, plane_b, h, j0, j1, True)
            multiply(codes_a, plane_a, h, j0, j1, False)
            nc.vector.tensor_copy(sums[h][:, j0:j1], banks[h][:, j0:j1])
        for h, j0, j1 in pieces:
            nc.scalar.activation(
                out=pages[h][:].indirect(idx_out[:, j0 // STRIPE : j1 // STRIPE]),
                in_=sums[h][:, j0:j1],
                func=COPY,
                scale=gain[:, 32 * h : 32 * h + 1],
            )
            if j1 == J:
                nc.sync.dma_start(out[h * P : (h + 1) * P, :], pages[h][:])
